import numpy as np
import ml_dtypes


def mxq(x, axis, fmt="e4m3"):
    dtype, down = {"e4m3": (ml_dtypes.float8_e4m3fn, 7), "e5m2": (ml_dtypes.float8_e5m2, 14)}[fmt]
    v = np.moveaxis(np.asarray(x, np.float32).astype(ml_dtypes.bfloat16).astype(np.float64), axis, -1)
    blocks = v.reshape(v.shape[:-1] + (-1, 32))
    amax = np.abs(blocks).max(-1, keepdims=True)
    byte = np.maximum(np.where(amax > 0, np.frexp(amax)[1] - 1 + 127, 0) - down, 1)
    scale = np.exp2(byte - 127.0)
    codes = (blocks / scale).astype(np.float32).astype(dtype).astype(np.float64)
    return np.moveaxis((codes * scale).reshape(v.shape), -1, axis)


WIDE = False


def mx_kscale(k):
    if not WIDE:
        return np.ones(k)
    levels = np.array([10, -10, 5, -5, 0])
    if k % 512:
        return np.exp2(np.random.permutation(np.resize(levels, k // 32))).repeat(32)
    a = np.empty((k // 512, 16))
    for p in range(k // 512):
        a[p, :8] = np.random.permutation(np.resize(levels, 8))
        for g in range(8):
            far = levels[np.abs(levels - a[p, g]) >= 10]
            a[p, g + 8] = far[np.random.randint(len(far))]
    return np.exp2(a.ravel()).repeat(32)


def f64(x):
    return np.asarray(x).astype(np.float64)


def striped(idx):
    return np.tile(idx.reshape(-1, 16).T, (8, 1)).astype(np.uint16)


def unstriped(offs):
    return offs[:16].T.reshape(-1).astype(np.int64)


E2M1 = np.array([0.0, 0.5, 1.0, 1.5, 2.0, 3.0, 4.0, 6.0, -0.0, -0.5, -1.0, -1.5, -2.0, -3.0, -4.0, -6.0])


def pack_weight(w, fmt):
    k, n = w.shape
    w = f64(np.asarray(w, np.float32).astype(ml_dtypes.bfloat16)).reshape(k // 32, 32, n)
    amax = np.abs(w).max(1)
    if fmt == "e4m3":
        byte = np.frexp(amax)[1] - 1 + 127 - 7
    else:
        mant, ex = np.frexp(amax / 6.0)
        byte = np.where(mant > 0.5, ex, ex - 1) + 127
    byte = np.clip(np.where(amax > 0, byte, 1), 1, 254)
    scaled = (w * np.exp2(127.0 - byte)[:, None, :]).reshape(k, n).astype(np.float32)
    by_word = np.ascontiguousarray(scaled.reshape(k // 512, 128, 4, n).transpose(0, 1, 3, 2))
    if fmt == "e4m3":
        words = by_word.astype(ml_dtypes.float8_e4m3fn).view(np.uint8)
    else:
        c = by_word.astype(ml_dtypes.float4_e2m1fn).view(np.uint8) & 0xF
        words = (c[..., 0::2] | (c[..., 1::2] << 4)).reshape(k // 512, 128, 2 * n)
    return np.ascontiguousarray(words), np.ascontiguousarray(byte.astype(np.uint8).reshape(k // 512, 16, n))


def unpack_weight(words, scales, fmt):
    g, _, n = scales.shape
    words = np.ascontiguousarray(words).reshape(g, 128, n, -1)
    if fmt == "e4m3":
        vals = words.view(ml_dtypes.float8_e4m3fn).astype(np.float64)
    else:
        nib = np.empty((g, 128, n, 4), np.uint8)
        nib[..., 0::2] = words & 0xF
        nib[..., 1::2] = words >> 4
        vals = E2M1[nib]
    vals = vals * np.repeat(np.exp2(scales.astype(np.float64) - 127.0), 8, axis=1)[..., None]
    return vals.transpose(0, 1, 3, 2).reshape(g * 512, n)


def gelu(v):
    return 0.5 * v * (1.0 + np.tanh(np.sqrt(2.0 / np.pi) * (v + 0.044715 * v**3)))


K, H, N, T, S, P, P2 = 1024, 1024, 512, 4096, 1024, 512, 256


def setup_inputs():
    n = np.random.standard_normal
    s = mx_kscale(K)[:, None]
    u = mx_kscale(H)[:, None]
    tab_words, tab_scales = pack_weight(n((K, T)) * s, "e4m3")
    w1 = 1.4 * n((K, H)) / np.sqrt(K) / s
    gain = np.exp(0.4 * n(H)) * u[:, 0]
    w4_words, w4_scales = pack_weight(n((H, N)) / np.sqrt(H) / u, "e2m1")
    masts = np.random.permutation(S)
    blocks = np.random.permutation(P)
    return {
        "tab_words": tab_words,
        "tab_scales": tab_scales,
        "offs": striped(np.random.permutation(T)[:S]),
        "w1": w1.astype(np.float32),
        "gain": gain.astype(np.float32),
        "pos1": striped(masts[:P]),
        "pos2": striped(masts[P:P + P]),
        "w4_words": w4_words,
        "w4_scales": w4_scales,
        "pos3": striped(blocks[:P2]),
        "pos4": striped(blocks[P2:P2 + P2]),
    }


def reference(tab_words, tab_scales, offs, w1, gain, pos1, pos2, w4_words, w4_scales, pos3, pos4):
    v = unpack_weight(tab_words, tab_scales, "e4m3")[:, unstriped(offs)]
    q1 = mxq(f64(w1), 0, "e4m3")
    h = f64(gain)[:, None] * np.tanh(q1.T @ v)
    x = np.abs(h[:, unstriped(pos1)] - h[:, unstriped(pos2)])
    w4 = unpack_weight(w4_words, w4_scales, "e2m1")
    y = w4.T @ mxq(x, 0, "e4m3")
    return np.maximum(y[:, unstriped(pos3)], y[:, unstriped(pos4)])

@@ -1,0 +1,279 @@
+from contextlib import ExitStack
+
+import concourse.mybir as mybir
+
+K, H, N, T, S, PAIRS, RIVALS = 1024, 1024, 512, 4096, 1024, 512, 256
+FLOPS = 2 * K * H * S + 2 * H * N * PAIRS
+
+F32 = mybir.dt.float32
+BF16 = mybir.dt.bfloat16
+I32 = mybir.dt.int32
+U32 = mybir.dt.uint32
+U16 = mybir.dt.uint16
+U8 = mybir.dt.uint8
+FP8X4 = mybir.dt.float8_e4m3fn_x4
+FP4X4 = mybir.dt.float4_e2m1fn_x4
+ALU = mybir.AluOpType
+ACT = mybir.ActivationFunctionType
+
+P = 128
+PACK = 4
+K_PASS = P * PACK
+BANK = 512
+HALF = 256
+
+
+def tile_list_frost_mast_contrast_kernel(
+    tc, tab_words, tab_scales, offs, w1, gain, pos1, pos2, w4_words, w4_scales, pos3, pos4, out
+):
+    nc = tc.nc
+    with ExitStack() as ctx:
+        lists = ctx.enter_context(tc.tile_pool(name="lists", bufs=1))
+        keep = ctx.enter_context(tc.tile_pool(name="keep", bufs=1))
+        ring = ctx.enter_context(tc.tile_pool(name="ring", bufs=3))
+        psum = ctx.enter_context(tc.psum_pool(name="psum", bufs=8))
+
+        def load_list(src, name):
+            t = lists.tile([P, src.shape[1]], U16, name=name)
+            nc.sync.dma_start(t[:], src)
+            return t
+
+        offs_sb = load_list(offs, "offs_sb")
+        tab_rows = keep.tile([P, T // 4], I32, name="tab_rows", align_bytes=64)
+        tab_sb = []
+        for a in range(2):
+            tab_sb.append(keep.tile([P, T], I32, name="tab_sb%d" % a, align_bytes=64))
+
+        def load_scale_rows(q):
+            for a in range(2):
+                nc.sync.dma_start(
+                    out=tab_rows[32 * q + 4 * a : 32 * q + 4 * a + 4, :],
+                    in_=tab_scales[a, 4 * q : 4 * q + 4, :].bitcast(I32),
+                )
+
+        def load_words(a):
+            nc.sync.dma_start(out=tab_sb[a][:], in_=tab_words[a].rearrange("p t i -> p (t i)").bitcast(I32))
+
+        load_scale_rows(0)
+        load_scale_rows(1)
+        load_scale_rows(2)
+        load_words(0)
+        load_scale_rows(3)
+        load_words(1)
+
+        raw = {}
+
+        def load_w1(b, a, c0, width):
+            t = keep.tile([P, PACK, width], F32, name="w1_raw", tag="raw%d%d%d" % (b, a, c0), align_bytes=64)
+            rows = w1[a * K_PASS : (a + 1) * K_PASS, b * K_PASS + c0 : b * K_PASS + c0 + width]
+            nc.sync.dma_start(out=t[:], in_=rows.rearrange("(p j) c -> p j c", j=PACK))
+            raw[b, a, c0] = t
+
+        for a in range(2):
+            load_w1(0, a, 0, HALF)
+            load_w1(0, a, HALF, HALF)
+        pos1_sb = load_list(pos1, "pos1_sb")
+        pos2_sb = load_list(pos2, "pos2_sb")
+        for a in range(2):
+            load_w1(1, a, 0, HALF)
+            load_w1(1, a, HALF, HALF)
+        gain_sb = keep.tile([P, 2, 8], F32, name="gain_sb")
+        nc.sync.dma_start(out=gain_sb[:, :, 0:PACK], in_=gain.rearrange("(b p t) -> p b t", b=2, t=PACK))
+        w4_sb = keep.tile([P, 2 * 2 * N], U8, name="w4_sb", align_bytes=64)
+        nc.sync.dma_start(
+            out=w4_sb[:].bitcast(I32).rearrange("p (a c) -> p a c", a=2),
+            in_=w4_words.bitcast(I32).rearrange("a p c -> p a c"),
+        )
+        pos3_sb = load_list(pos3, "pos3_sb")
+        pos4_sb = load_list(pos4, "pos4_sb")
+
+        w4_plane = keep.tile([P, 2 * N], U8, name="w4_plane", align_bytes=64)
+        tab_plane = keep.tile([P, T], U8, name="tab_plane", align_bytes=64)
+        nc.vector.memset(tab_plane[:].bitcast(I32), 0)
+        nc.vector.memset(w4_plane[:].bitcast(I32), 0)
+        for q in range(4):
+            nc.sync.dma_start(
+                out=w4_plane[32 * q : 32 * q + 4, :].bitcast(I32).rearrange("r (a c) -> r a c", a=2),
+                in_=w4_scales[:, 4 * q : 4 * q + 4, :].bitcast(I32).rearrange("a r c -> r a c"),
+            )
+        for q in range(4):
+            nc.vector.tensor_copy(tab_plane[32 * q : 32 * q + 8, :].bitcast(I32), tab_rows[32 * q : 32 * q + 8, :])
+
+        v_plane = keep.tile([P, S], U8, name="v_plane", align_bytes=64)
+        nc.vector.tensor_copy(v_plane[:], tab_plane[:].indirect(offs_sb[:]))
+        v_words = []
+        for a in range(2):
+            t = keep.tile([P, S], U32, name="v_words%d" % a, align_bytes=64)
+            nc.vector.tensor_copy(t[:], tab_sb[a][:].bitcast(U32).indirect(offs_sb[:]))
+            v_words.append(t)
+
+        grouped, w1_codes, w1_plane = {}, {}, {}
+        for b in range(2):
+            for a in range(2):
+                grouped[b, a] = keep.tile([P, PACK * K_PASS], BF16, name="w1_grouped%d%d" % (b, a), align_bytes=64)
+                w1_codes[b, a] = keep.tile([P, K_PASS], U32, name="w1_codes%d%d" % (b, a), align_bytes=64)
+                w1_plane[b, a] = keep.tile([P, K_PASS], U8, name="w1_plane%d%d" % (b, a), align_bytes=64)
+
+        def round_w1(b, a, tile_c0, on_vector, lo=0, hi=HALF):
+            src = raw[b, a, tile_c0][:, :, lo:hi].rearrange("p j (m t) -> p m j t", t=PACK)
+            m0, m1 = (tile_c0 + lo) // PACK, (tile_c0 + hi) // PACK
+            dst = grouped[b, a][:].rearrange("p (t m j) -> p m j t", t=PACK, j=PACK)[:, m0:m1]
+            if on_vector:
+                nc.vector.tensor_copy(out=dst, in_=src)
+            else:
+                nc.scalar.copy(out=dst, in_=src)
+
+        def quantise_w1(b, a, t0, t1):
+            nc.vector.quantize_mx(
+                out=w1_codes[b, a][:, t0 * P : t1 * P].bitcast(FP8X4),
+                scales=w1_plane[b, a][:, t0 * P : t1 * P],
+                in_=grouped[b, a][:, t0 * K_PASS : t1 * K_PASS],
+            )
+
+        h = {}
+
+        def first_product(i, tag):
+            b, t = divmod(i, PACK)
+            h[i] = keep.tile([P, S], F32, name="h", tag=tag, align_bytes=64)
+            for c0 in range(0, S, BANK):
+                acc = psum.tile([P, BANK], F32, name="acc")
+                for a in range(2):
+                    nc.tensor.matmul_mx(
+                        out=acc[:],
+                        lhsT=w1_codes[b, a][:, t * P : (t + 1) * P].bitcast(FP8X4),
+                        lhsT_scale=w1_plane[b, a][:, t * P : (t + 1) * P],
+                        rhs=v_words[a][:, c0 : c0 + BANK].bitcast(FP8X4),
+                        rhs_scale=v_plane[4 * a : P, c0 : c0 + BANK],
+                        start=(a == 0),
+                        stop=(a == 1),
+                    )
+                nc.scalar.activation(out=h[i][:, c0 : c0 + BANK], in_=acc[:], func=ACT.Tanh)
+
+        round_w1(0, 0, 0, False)
+        round_w1(0, 0, HALF, True)
+        quantise_w1(0, 0, 0, 4)
+        round_w1(0, 1, 0, False)
+        round_w1(0, 1, HALF, True, 0, 160)
+        round_w1(0, 1, HALF, False, 160, HALF)
+        quantise_w1(0, 1, 0, 1)
+        quantise_w1(0, 1, 1, 4)
+        first_product(0, "h0")
+        first_product(1, "h1")
+        for a in range(2):
+            round_w1(1, a, 0, False)
+            round_w1(1, a, HALF, False)
+            quantise_w1(1, a, 0, 4)
+            first_product(2 + a, "raw1%d%d" % (a, HALF))
+        for i in range(4, 8):
+            first_product(i, "h%d" % i)
+
+        diff = [keep.tile([P, PAIRS], F32, name="diff%d" % i) for i in range(8)]
+        chunks = [(0, HALF), (HALF, P), (HALF + P, P)]
+        steps = [(i, c0, HALF) for i in range(6) for c0 in (0, HALF)]
+        steps = steps + [(i, c0, width) for c0, width in chunks for i in (6, 7)]
+        first = {}
+
+        def pick_first(i, c0, width):
+            first[i, c0] = ring.tile([P, HALF], F32, name="first")
+            nc.vector.tensor_copy(first[i, c0][:, 0:width], h[i][:].indirect(pos1_sb[:, c0 // 16 : (c0 + width) // 16]))
+
+        def pick_second(i, c0, width):
+            nc.vector.tensor_tensor(
+                diff[i][:, c0 : c0 + width],
+                h[i][:].indirect(pos2_sb[:, c0 // 16 : (c0 + width) // 16]),
+                first[i, c0][:, 0:width],
+                ALU.subtract,
+            )
+
+        pick_first(*steps[0])
+        for k in range(1, len(steps)):
+            pick_first(*steps[k])
+            pick_second(*steps[k - 1])
+        pick_second(*steps[-1])
+
+        x_rows = [
+            keep.tile([P, PACK, PAIRS], BF16, name="x_rows", tag="raw110", align_bytes=64),
+            keep.tile([P, PACK, PAIRS], BF16, name="x_rows1", align_bytes=64),
+        ]
+        x_grouped = [keep.tile([P, PAIRS * PACK], BF16, name="x_grouped%d" % b, align_bytes=64) for b in range(2)]
+        x_codes = [keep.tile([P, PAIRS], U32, name="x_codes%d" % b, align_bytes=64) for b in range(2)]
+        x_plane = [keep.tile([P, PAIRS], U8, name="x_plane%d" % b, align_bytes=64) for b in range(2)]
+
+        def scale_abs(i, c0, width):
+            b, t = divmod(i, PACK)
+            nc.scalar.activation(
+                out=x_rows[b][:, t, c0 : c0 + width],
+                in_=diff[i][:, c0 : c0 + width],
+                func=ACT.Abs,
+                scale=gain_sb[:, b, t : t + 1],
+            )
+
+        def scale_abs_woven(i, c0, width):
+            b, t = divmod(i, PACK)
+            nc.scalar.activation(
+                out=x_grouped[b][:].rearrange("p (m t) -> p m t", t=PACK)[:, c0 : c0 + width, t],
+                in_=diff[i][:, c0 : c0 + width],
+                func=ACT.Abs,
+                scale=gain_sb[:, b, t : t + 1],
+            )
+
+        def weave_x(b, c0, width, rows=PACK):
+            src = x_rows[b][:, 0:rows, c0 : c0 + width].rearrange("p t (c i) -> p c t i", i=4)
+            dst = x_grouped[b][:, c0 * PACK : (c0 + width) * PACK].rearrange("p (c i t) -> p c t i", i=4, t=PACK)
+            nc.scalar.copy(out=dst[:, :, 0:rows, :], in_=src)
+
+        def quantise_x(b, c0, width):
+            nc.vector.quantize_mx(
+                out=x_codes[b][:, c0 : c0 + width].bitcast(FP8X4),
+                scales=x_plane[b][:, c0 : c0 + width],
+                in_=x_grouped[b][:, c0 * PACK : (c0 + width) * PACK],
+            )
+
+        for i in range(4):
+            scale_abs(i, 0, PAIRS)
+        weave_x(0, 0, HALF)
+        weave_x(0, HALF, HALF)
+        quantise_x(0, 0, PAIRS)
+        for i in range(4, 6):
+            scale_abs(i, 0, PAIRS)
+        weave_x(1, *chunks[-1], rows=2)
+        for c0, width in chunks[:-1]:
+            scale_abs(6, c0, width)
+            scale_abs(7, c0, width)
+            weave_x(1, c0, width)
+            quantise_x(1, c0, width)
+        scale_abs_woven(6, *chunks[-1])
+        scale_abs_woven(7, *chunks[-1])
+        quantise_x(1, *chunks[-1])
+
+        def second_pass(acc, n, b, c0, width, start, stop):
+            nc.tensor.matmul_mx(
+                out=acc,
+                lhsT=w4_sb[:, 2 * (b * N + n * P) : 2 * (b * N + (n + 1) * P)].bitcast(FP4X4),
+                lhsT_scale=w4_plane[:, b * N + n * P : b * N + (n + 1) * P],
+                rhs=x_codes[b][:, c0 : c0 + width].bitcast(FP8X4),
+                rhs_scale=x_plane[b][:, c0 : c0 + width],
+                start=start,
+                stop=stop,
+            )
+
+        for n in range(N // P):
+            y = keep.tile([P, PAIRS], F32, name="y%d" % n)
+            if n == 0:
+                for c0, width in chunks:
+                    acc = psum.tile([P, BANK], F32, name="acc")
+                    second_pass(acc[:, 0:width], n, 0, c0, width, True, False)
+                    second_pass(acc[:, 0:width], n, 1, c0, width, False, True)
+                    nc.scalar.copy(out=y[:, c0 : c0 + width], in_=acc[:, 0:width])
+            else:
+                acc = psum.tile([P, BANK], F32, name="acc")
+                second_pass(acc[:], n, 0, 0, PAIRS, True, False)
+                second_pass(acc[:], n, 1, 0, PAIRS, False, True)
+                nc.scalar.copy(out=y[:], in_=acc[:])
+            rival_a = keep.tile([P, RIVALS], F32, name="rival_a%d" % n)
+            rival_b = keep.tile([P, RIVALS], F32, name="rival_b%d" % n)
+            best = keep.tile([P, RIVALS], F32, name="best%d" % n)
+            nc.vector.tensor_copy(rival_a[:], y[:].indirect(pos3_sb[:]))
+            nc.vector.tensor_copy(rival_b[:], y[:].indirect(pos4_sb[:]))
+            nc.vector.tensor_tensor(best[:], rival_a[:], rival_b[:], ALU.max)
+            nc.sync.dma_start(out=out[n * P : (n + 1) * P, :], in_=best[:])

@@ -30,7 +30,7 @@ def tile_list_frost_mast_contrast_kernel(
     with ExitStack() as ctx:
         lists = ctx.enter_context(tc.tile_pool(name="lists", bufs=1))
         keep = ctx.enter_context(tc.tile_pool(name="keep", bufs=1))
-        ring = ctx.enter_context(tc.tile_pool(name="ring", bufs=3))
+        ring = ctx.enter_context(tc.tile_pool(name="ring", bufs=2))
         psum = ctx.enter_context(tc.psum_pool(name="psum", bufs=8))
 
         def load_list(src, name):
@@ -59,7 +59,6 @@ def tile_list_frost_mast_contrast_kernel(
         load_scale_rows(2)
         load_words(0)
         load_scale_rows(3)
-        load_words(1)
 
         raw = {}
 
@@ -69,14 +68,12 @@ def tile_list_frost_mast_contrast_kernel(
             nc.sync.dma_start(out=t[:], in_=rows.rearrange("(p j) c -> p j c", j=PACK))
             raw[b, a, c0] = t
 
-        for a in range(2):
-            load_w1(0, a, 0, HALF)
-            load_w1(0, a, HALF, HALF)
+        load_w1(0, 0, 0, K_PASS)
+        load_words(1)
+        load_w1(0, 1, 0, HALF)
+        load_w1(0, 1, HALF, HALF)
         pos1_sb = load_list(pos1, "pos1_sb")
         pos2_sb = load_list(pos2, "pos2_sb")
-        for a in range(2):
-            load_w1(1, a, 0, HALF)
-            load_w1(1, a, HALF, HALF)
         gain_sb = keep.tile([P, 2, 8], F32, name="gain_sb")
         nc.sync.dma_start(out=gain_sb[:, :, 0:PACK], in_=gain.rearrange("(b p t) -> p b t", b=2, t=PACK))
         w4_sb = keep.tile([P, 2 * 2 * N], U8, name="w4_sb", align_bytes=64)
@@ -84,6 +81,8 @@ def tile_list_frost_mast_contrast_kernel(
             out=w4_sb[:].bitcast(I32).rearrange("p (a c) -> p a c", a=2),
             in_=w4_words.bitcast(I32).rearrange("a p c -> p a c"),
         )
+        for a in range(2):
+            load_w1(1, a, 0, K_PASS)
         pos3_sb = load_list(pos3, "pos3_sb")
         pos4_sb = load_list(pos4, "pos4_sb")
 
@@ -115,9 +114,9 @@ def tile_list_frost_mast_contrast_kernel(
                 w1_plane[b, a] = keep.tile([P, K_PASS], U8, name="w1_plane%d%d" % (b, a), align_bytes=64)
 
         def round_w1(b, a, tile_c0, on_vector, lo=0, hi=HALF):
-            src = raw[b, a, tile_c0][:, :, lo:hi].rearrange("p j (m t) -> p m j t", t=PACK)
+            src = raw[b, a, tile_c0][:, :, lo:hi].rearrange("p j (m t) -> p m t j", t=PACK)
             m0, m1 = (tile_c0 + lo) // PACK, (tile_c0 + hi) // PACK
-            dst = grouped[b, a][:].rearrange("p (t m j) -> p m j t", t=PACK, j=PACK)[:, m0:m1]
+            dst = grouped[b, a][:].rearrange("p (t m j) -> p m t j", t=PACK, j=PACK)[:, m0:m1]
             if on_vector:
                 nc.vector.tensor_copy(out=dst, in_=src)
             else:
@@ -150,7 +149,7 @@ def tile_list_frost_mast_contrast_kernel(
                 nc.scalar.activation(out=h[i][:, c0 : c0 + BANK], in_=acc[:], func=ACT.Tanh)
 
         round_w1(0, 0, 0, False)
-        round_w1(0, 0, HALF, True)
+        round_w1(0, 0, 0, False, HALF, K_PASS)
         quantise_w1(0, 0, 0, 4)
         round_w1(0, 1, 0, False)
         round_w1(0, 1, HALF, True, 0, 160)
@@ -161,66 +160,39 @@ def tile_list_frost_mast_contrast_kernel(
         first_product(1, "h1")
         for a in range(2):
             round_w1(1, a, 0, False)
-            round_w1(1, a, HALF, False)
+            round_w1(1, a, 0, False, HALF, K_PASS)
             quantise_w1(1, a, 0, 4)
-            first_product(2 + a, "raw1%d%d" % (a, HALF))
+            first_product(2 + a, "raw1%d0" % a)
         for i in range(4, 8):
             first_product(i, "h%d" % i)
 
-        diff = [keep.tile([P, PAIRS], F32, name="diff%d" % i) for i in range(8)]
-        chunks = [(0, HALF), (HALF, P), (HALF + P, P)]
-        steps = [(i, c0, HALF) for i in range(6) for c0 in (0, HALF)]
-        steps = steps + [(i, c0, width) for c0, width in chunks for i in (6, 7)]
-        first = {}
-
-        def pick_first(i, c0, width):
-            first[i, c0] = ring.tile([P, HALF], F32, name="first")
-            nc.vector.tensor_copy(first[i, c0][:, 0:width], h[i][:].indirect(pos1_sb[:, c0 // 16 : (c0 + width) // 16]))
-
-        def pick_second(i, c0, width):
-            nc.vector.tensor_tensor(
-                diff[i][:, c0 : c0 + width],
-                h[i][:].indirect(pos2_sb[:, c0 // 16 : (c0 + width) // 16]),
-                first[i, c0][:, 0:width],
-                ALU.subtract,
-            )
-
-        pick_first(*steps[0])
-        for k in range(1, len(steps)):
-            pick_first(*steps[k])
-            pick_second(*steps[k - 1])
-        pick_second(*steps[-1])
-
-        x_rows = [
-            keep.tile([P, PACK, PAIRS], BF16, name="x_rows", tag="raw110", align_bytes=64),
-            keep.tile([P, PACK, PAIRS], BF16, name="x_rows1", align_bytes=64),
+        x_rows = [keep.tile([P, PACK, PAIRS], F32, name="x_rows%d" % b, align_bytes=64) for b in range(2)]
+        x_grouped = [
+            keep.tile([P, PAIRS * PACK], BF16, name="x_grouped", tag="x_grouped%d" % b, align_bytes=64) for b in range(2)
         ]
-        x_grouped = [keep.tile([P, PAIRS * PACK], BF16, name="x_grouped%d" % b, align_bytes=64) for b in range(2)]
         x_codes = [keep.tile([P, PAIRS], U32, name="x_codes%d" % b, align_bytes=64) for b in range(2)]
         x_plane = [keep.tile([P, PAIRS], U8, name="x_plane%d" % b, align_bytes=64) for b in range(2)]
+        chunks = [(0, HALF), (HALF, P), (HALF + P, P)]
 
-        def scale_abs(i, c0, width):
-            b, t = divmod(i, PACK)
-            nc.scalar.activation(
-                out=x_rows[b][:, t, c0 : c0 + width],
-                in_=diff[i][:, c0 : c0 + width],
-                func=ACT.Abs,
-                scale=gain_sb[:, b, t : t + 1],
-            )
+        def two_differences(steps):
+            firsts = []
+            for i, c0, width, dst in steps:
+                first = ring.tile([P, HALF], F32, name="first")
+                nc.vector.tensor_copy(first[:, 0:width], h[i][:].indirect(pos1_sb[:, c0 // 16 : (c0 + width) // 16]))
+                firsts.append(first)
+            for first, (i, c0, width, dst) in zip(firsts, steps):
+                nc.vector.tensor_tensor(
+                    dst, h[i][:].indirect(pos2_sb[:, c0 // 16 : (c0 + width) // 16]), first[:, 0:width], ALU.subtract
+                )
 
-        def scale_abs_woven(i, c0, width):
+        def scale_abs(dst, src, i):
             b, t = divmod(i, PACK)
-            nc.scalar.activation(
-                out=x_grouped[b][:].rearrange("p (m t) -> p m t", t=PACK)[:, c0 : c0 + width, t],
-                in_=diff[i][:, c0 : c0 + width],
-                func=ACT.Abs,
-                scale=gain_sb[:, b, t : t + 1],
-            )
+            nc.scalar.activation(out=dst, in_=src, func=ACT.Abs, scale=gain_sb[:, b, t : t + 1])
 
         def weave_x(b, c0, width, rows=PACK):
             src = x_rows[b][:, 0:rows, c0 : c0 + width].rearrange("p t (c i) -> p c t i", i=4)
             dst = x_grouped[b][:, c0 * PACK : (c0 + width) * PACK].rearrange("p (c i t) -> p c t i", i=4, t=PACK)
-            nc.scalar.copy(out=dst[:, :, 0:rows, :], in_=src)
+            nc.scalar.activation(out=dst[:, :, 0:rows, :], in_=src, func=ACT.Abs)
 
         def quantise_x(b, c0, width):
             nc.vector.quantize_mx(
@@ -229,22 +201,30 @@ def tile_list_frost_mast_contrast_kernel(
                 in_=x_grouped[b][:, c0 * PACK : (c0 + width) * PACK],
             )
 
-        for i in range(4):
-            scale_abs(i, 0, PAIRS)
+        for i in range(6):
+            b, t = divmod(i, PACK)
+            diff = keep.tile([P, PAIRS], F32, name="diff%d" % i)
+            two_differences([(i, c0, HALF, diff[:, c0 : c0 + HALF]) for c0 in (0, HALF)])
+            nc.gpsimd.tensor_scalar(x_rows[b][:, t, :], diff[:], gain_sb[:, b, t : t + 1], 0.0, ALU.mult, ALU.add)
         weave_x(0, 0, HALF)
         weave_x(0, HALF, HALF)
         quantise_x(0, 0, PAIRS)
-        for i in range(4, 6):
-            scale_abs(i, 0, PAIRS)
         weave_x(1, *chunks[-1], rows=2)
-        for c0, width in chunks[:-1]:
-            scale_abs(6, c0, width)
-            scale_abs(7, c0, width)
-            weave_x(1, c0, width)
+        for k, (c0, width) in enumerate(chunks):
+            late = {}
+            for i in (6, 7):
+                tag = "x_grouped0" if (k, i) == (1, 6) else "late%d%d" % (k, i)
+                late[i] = keep.tile([P, width], F32, name="late", tag=tag, align_bytes=64)
+            two_differences([(i, c0, width, late[i][:]) for i in (6, 7)])
+            for i in (6, 7):
+                if k < len(chunks) - 1:
+                    scale_abs(x_rows[1][:, i - PACK, c0 : c0 + width], late[i][:], i)
+                else:
+                    woven = x_grouped[1][:].rearrange("p (m t) -> p m t", t=PACK)
+                    scale_abs(woven[:, c0 : c0 + width, i - PACK], late[i][:], i)
+            if k < len(chunks) - 1:
+                weave_x(1, c0, width)
             quantise_x(1, c0, width)
-        scale_abs_woven(6, *chunks[-1])
-        scale_abs_woven(7, *chunks[-1])
-        quantise_x(1, *chunks[-1])
 
         def second_pass(acc, n, b, c0, width, start, stop):
             nc.tensor.matmul_mx(

@@ -45,20 +45,14 @@ def tile_list_frost_mast_contrast_kernel(
             tab_sb.append(keep.tile([P, T], I32, name="tab_sb%d" % a, align_bytes=64))
 
         def load_scale_rows(q):
-            for a in range(2):
-                nc.sync.dma_start(
-                    out=tab_rows[32 * q + 4 * a : 32 * q + 4 * a + 4, :],
-                    in_=tab_scales[a, 4 * q : 4 * q + 4, :].bitcast(I32),
-                )
+            nc.sync.dma_start(out=tab_rows[32 * q : 32 * q + 8, :], in_=tab_scales[:, 4 * q : 4 * q + 4, :].bitcast(I32))
 
         def load_words(a):
             nc.sync.dma_start(out=tab_sb[a][:], in_=tab_words[a].rearrange("p t i -> p (t i)").bitcast(I32))
 
-        load_scale_rows(0)
-        load_scale_rows(1)
-        load_scale_rows(2)
+        for q in range(4):
+            load_scale_rows(q)
         load_words(0)
-        load_scale_rows(3)
 
         raw = {}
 
@@ -70,10 +64,13 @@ def tile_list_frost_mast_contrast_kernel(
 
         load_w1(0, 0, 0, K_PASS)
         load_words(1)
-        load_w1(0, 1, 0, HALF)
-        load_w1(0, 1, HALF, HALF)
         pos1_sb = load_list(pos1, "pos1_sb")
         pos2_sb = load_list(pos2, "pos2_sb")
+        load_w1(0, 1, 0, HALF)
+        load_w1(0, 1, HALF, HALF)
+        load_w1(1, 0, 0, HALF)
+        load_w1(1, 0, HALF, HALF)
+        load_w1(1, 1, 0, K_PASS)
         gain_sb = keep.tile([P, 2, 8], F32, name="gain_sb")
         nc.sync.dma_start(out=gain_sb[:, :, 0:PACK], in_=gain.rearrange("(b p t) -> p b t", b=2, t=PACK))
         w4_sb = keep.tile([P, 2 * 2 * N], U8, name="w4_sb", align_bytes=64)
@@ -81,8 +78,6 @@ def tile_list_frost_mast_contrast_kernel(
             out=w4_sb[:].bitcast(I32).rearrange("p (a c) -> p a c", a=2),
             in_=w4_words.bitcast(I32).rearrange("a p c -> p a c"),
         )
-        for a in range(2):
-            load_w1(1, a, 0, K_PASS)
         pos3_sb = load_list(pos3, "pos3_sb")
         pos4_sb = load_list(pos4, "pos4_sb")
 
@@ -109,7 +104,9 @@ def tile_list_frost_mast_contrast_kernel(
         grouped, w1_codes, w1_plane = {}, {}, {}
         for b in range(2):
             for a in range(2):
-                grouped[b, a] = keep.tile([P, PACK * K_PASS], BF16, name="w1_grouped%d%d" % (b, a), align_bytes=64)
+                grouped[b, a] = keep.tile(
+                    [P, PACK * K_PASS], BF16, name="w1_grouped", tag="grouped%d%d" % (b, a), align_bytes=64
+                )
                 w1_codes[b, a] = keep.tile([P, K_PASS], U32, name="w1_codes%d%d" % (b, a), align_bytes=64)
                 w1_plane[b, a] = keep.tile([P, K_PASS], U8, name="w1_plane%d%d" % (b, a), align_bytes=64)
 
@@ -156,23 +153,24 @@ def tile_list_frost_mast_contrast_kernel(
         round_w1(0, 1, HALF, False, 160, HALF)
         quantise_w1(0, 1, 0, 1)
         quantise_w1(0, 1, 1, 4)
+        round_w1(1, 0, 0, True)
         first_product(0, "h0")
         first_product(1, "h1")
-        for a in range(2):
-            round_w1(1, a, 0, False)
-            round_w1(1, a, 0, False, HALF, K_PASS)
-            quantise_w1(1, a, 0, 4)
-            first_product(2 + a, "raw1%d0" % a)
-        for i in range(4, 8):
+        round_w1(1, 0, HALF, False)
+        quantise_w1(1, 0, 0, 4)
+        first_product(2, "raw10%d" % HALF)
+        round_w1(1, 1, 0, False)
+        round_w1(1, 1, 0, False, HALF, K_PASS)
+        quantise_w1(1, 1, 0, 4)
+        first_product(3, "raw110")
+        for i in (4, 6, 5, 7):
             first_product(i, "h%d" % i)
 
-        x_rows = [keep.tile([P, PACK, PAIRS], F32, name="x_rows%d" % b, align_bytes=64) for b in range(2)]
-        x_grouped = [
-            keep.tile([P, PAIRS * PACK], BF16, name="x_grouped", tag="x_grouped%d" % b, align_bytes=64) for b in range(2)
-        ]
+        chunks = [(0, HALF), (HALF, P), (HALF + P, P)]
+        upper = 2 * PAIRS + chunks[-1][0]
+        x_rows = {}
         x_codes = [keep.tile([P, PAIRS], U32, name="x_codes%d" % b, align_bytes=64) for b in range(2)]
         x_plane = [keep.tile([P, PAIRS], U8, name="x_plane%d" % b, align_bytes=64) for b in range(2)]
-        chunks = [(0, HALF), (HALF, P), (HALF + P, P)]
 
         def two_differences(steps):
             firsts = []
@@ -189,42 +187,48 @@ def tile_list_frost_mast_contrast_kernel(
             b, t = divmod(i, PACK)
             nc.scalar.activation(out=dst, in_=src, func=ACT.Abs, scale=gain_sb[:, b, t : t + 1])
 
-        def weave_x(b, c0, width, rows=PACK):
-            src = x_rows[b][:, 0:rows, c0 : c0 + width].rearrange("p t (c i) -> p c t i", i=4)
-            dst = x_grouped[b][:, c0 * PACK : (c0 + width) * PACK].rearrange("p (c i t) -> p c t i", i=4, t=PACK)
-            nc.scalar.activation(out=dst[:, :, 0:rows, :], in_=src, func=ACT.Abs)
+        def weave_x(dst, b, c0, width, pitch, copy=nc.scalar.copy):
+            rows = x_rows[b][:, c0 : c0 + 2 * pitch].rearrange("p (u r) -> p u r", u=2)[:, :, 0 : 2 * PAIRS]
+            src = rows.rearrange("p u (l m) -> p u l m", l=2)[:, :, :, 0:width].rearrange("p u l (c i) -> p c u l i", i=4)
+            copy(out=dst.rearrange("p (c i u l) -> p c u l i", i=4, u=2, l=2), in_=src)
 
-        def quantise_x(b, c0, width):
+        def quantise_x(src, b, c0, width):
             nc.vector.quantize_mx(
-                out=x_codes[b][:, c0 : c0 + width].bitcast(FP8X4),
-                scales=x_plane[b][:, c0 : c0 + width],
-                in_=x_grouped[b][:, c0 * PACK : (c0 + width) * PACK],
+                out=x_codes[b][:, c0 : c0 + width].bitcast(FP8X4), scales=x_plane[b][:, c0 : c0 + width], in_=src
             )
 
+        x_grouped = keep.tile([P, PAIRS * PACK], BF16, name="x_grouped", tag="x_grouped", align_bytes=64)
         for i in range(6):
             b, t = divmod(i, PACK)
+            if t == 0:
+                x_rows[b] = keep.tile([P, 2 * upper], F32, name="x_rows", tag="x_rows", align_bytes=64)
             diff = keep.tile([P, PAIRS], F32, name="diff%d" % i)
             two_differences([(i, c0, HALF, diff[:, c0 : c0 + HALF]) for c0 in (0, HALF)])
-            nc.gpsimd.tensor_scalar(x_rows[b][:, t, :], diff[:], gain_sb[:, b, t : t + 1], 0.0, ALU.mult, ALU.add)
-        weave_x(0, 0, HALF)
-        weave_x(0, HALF, HALF)
-        quantise_x(0, 0, PAIRS)
-        weave_x(1, *chunks[-1], rows=2)
+            row = x_rows[b][:, t * PAIRS : (t + 1) * PAIRS]
+            if b == 0:
+                nc.gpsimd.tensor_scalar(row, diff[:], gain_sb[:, b, t : t + 1], 0.0, ALU.mult, ALU.add)
+            else:
+                scale_abs(row, diff[:], i)
+            if i == PACK - 1:
+                rows = x_rows[0][:, 0 : PACK * PAIRS].rearrange("p (t m) -> p t m", t=PACK)
+                for c0 in (0, HALF):
+                    nc.scalar.activation(
+                        out=x_grouped[:, c0 * PACK : (c0 + HALF) * PACK].rearrange("p (c i t) -> p c t i", i=4, t=PACK),
+                        in_=rows[:, :, c0 : c0 + HALF].rearrange("p t (c i) -> p c t i", i=4),
+                        func=ACT.Abs,
+                    )
+        quantise_x(x_grouped[:], 0, 0, PAIRS)
+        late_tags = ["late0", "x_grouped", "woven0"]
         for k, (c0, width) in enumerate(chunks):
-            late = {}
+            pair = keep.tile([P, 2 * width], F32, name="late", tag=late_tags[k], align_bytes=64)
+            late = {i: pair[:, (i - 6) * width : (i - 5) * width] for i in (6, 7)}
+            two_differences([(i, c0, width, late[i]) for i in (6, 7)])
             for i in (6, 7):
-                tag = "x_grouped0" if (k, i) == (1, 6) else "late%d%d" % (k, i)
-                late[i] = keep.tile([P, width], F32, name="late", tag=tag, align_bytes=64)
-            two_differences([(i, c0, width, late[i][:]) for i in (6, 7)])
-            for i in (6, 7):
-                if k < len(chunks) - 1:
-                    scale_abs(x_rows[1][:, i - PACK, c0 : c0 + width], late[i][:], i)
-                else:
-                    woven = x_grouped[1][:].rearrange("p (m t) -> p m t", t=PACK)
-                    scale_abs(woven[:, c0 : c0 + width, i - PACK], late[i][:], i)
-            if k < len(chunks) - 1:
-                weave_x(1, c0, width)
-            quantise_x(1, c0, width)
+                row = upper + (i - 6) * PAIRS
+                scale_abs(x_rows[1][:, row : row + width], late[i], i)
+            woven = keep.tile([P, width * PACK], BF16, name="woven", tag="woven%d" % k, align_bytes=64)
+            weave_x(woven[:], 1, c0, width, upper - c0, nc.vector.tensor_copy if k == len(chunks) - 1 else nc.scalar.copy)
+            quantise_x(woven[:], 1, c0, width)
 
         def second_pass(acc, n, b, c0, width, start, stop):
             nc.tensor.matmul_mx(
@@ -240,11 +244,13 @@ def tile_list_frost_mast_contrast_kernel(
         for n in range(N // P):
             y = keep.tile([P, PAIRS], F32, name="y%d" % n)
             if n == 0:
-                for c0, width in chunks:
+                for part in (chunks[:-1], chunks[-1:]):
                     acc = psum.tile([P, BANK], F32, name="acc")
-                    second_pass(acc[:, 0:width], n, 0, c0, width, True, False)
-                    second_pass(acc[:, 0:width], n, 1, c0, width, False, True)
-                    nc.scalar.copy(out=y[:, c0 : c0 + width], in_=acc[:, 0:width])
+                    passes = [(b, c0, width) for b in range(2) for c0, width in part]
+                    for k, (b, c0, width) in enumerate(passes):
+                        second_pass(acc[:, c0 : c0 + width], n, b, c0, width, k == 0, k == len(passes) - 1)
+                    lo, hi = part[0][0], part[-1][0] + part[-1][1]
+                    nc.scalar.copy(out=y[:, lo:hi], in_=acc[:, lo:hi])
             else:
                 acc = psum.tile([P, BANK], F32, name="acc")
                 second_pass(acc[:], n, 0, 0, PAIRS, True, False)

@@ -30,7 +30,6 @@ def tile_list_frost_mast_contrast_kernel(
     with ExitStack() as ctx:
         lists = ctx.enter_context(tc.tile_pool(name="lists", bufs=1))
         keep = ctx.enter_context(tc.tile_pool(name="keep", bufs=1))
-        ring = ctx.enter_context(tc.tile_pool(name="ring", bufs=2))
         psum = ctx.enter_context(tc.psum_pool(name="psum", bufs=8))
 
         def load_list(src, name):
@@ -45,14 +44,20 @@ def tile_list_frost_mast_contrast_kernel(
             tab_sb.append(keep.tile([P, T], I32, name="tab_sb%d" % a, align_bytes=64))
 
         def load_scale_rows(q):
-            nc.sync.dma_start(out=tab_rows[32 * q : 32 * q + 8, :], in_=tab_scales[:, 4 * q : 4 * q + 4, :].bitcast(I32))
+            for a in range(2):
+                nc.sync.dma_start(
+                    out=tab_rows[32 * q + 4 * a : 32 * q + 4 * a + 4, :],
+                    in_=tab_scales[a, 4 * q : 4 * q + 4, :].bitcast(I32),
+                )
 
         def load_words(a):
             nc.sync.dma_start(out=tab_sb[a][:], in_=tab_words[a].rearrange("p t i -> p (t i)").bitcast(I32))
 
-        for q in range(4):
-            load_scale_rows(q)
+        load_scale_rows(0)
+        load_scale_rows(2)
+        load_scale_rows(1)
         load_words(0)
+        load_scale_rows(3)
 
         raw = {}
 
@@ -175,7 +180,7 @@ def tile_list_frost_mast_contrast_kernel(
         def two_differences(steps):
             firsts = []
             for i, c0, width, dst in steps:
-                first = ring.tile([P, HALF], F32, name="first")
+                first = keep.tile([P, HALF], F32, name="first", tag="h%d" % (11 - i), align_bytes=64)
                 nc.vector.tensor_copy(first[:, 0:width], h[i][:].indirect(pos1_sb[:, c0 // 16 : (c0 + width) // 16]))
                 firsts.append(first)
             for first, (i, c0, width, dst) in zip(firsts, steps):
@@ -203,20 +208,17 @@ def tile_list_frost_mast_contrast_kernel(
             if t == 0:
                 x_rows[b] = keep.tile([P, 2 * upper], F32, name="x_rows", tag="x_rows", align_bytes=64)
             diff = keep.tile([P, PAIRS], F32, name="diff%d" % i)
-            two_differences([(i, c0, HALF, diff[:, c0 : c0 + HALF]) for c0 in (0, HALF)])
+            picked = []
+            for which, pos in enumerate((pos1_sb, pos2_sb)):
+                tag = "picked%d%d" % (i, which)
+                picked.append(keep.tile([P, PAIRS], F32, name="picked", tag=tag, align_bytes=64))
+                nc.vector.tensor_copy(picked[which][:], h[i][:].indirect(pos[:]))
+            nc.gpsimd.tensor_tensor(diff[:], picked[0][:], picked[1][:], ALU.subtract)
             row = x_rows[b][:, t * PAIRS : (t + 1) * PAIRS]
-            if b == 0:
-                nc.gpsimd.tensor_scalar(row, diff[:], gain_sb[:, b, t : t + 1], 0.0, ALU.mult, ALU.add)
-            else:
-                scale_abs(row, diff[:], i)
+            scale_abs(row, diff[:], i)
             if i == PACK - 1:
-                rows = x_rows[0][:, 0 : PACK * PAIRS].rearrange("p (t m) -> p t m", t=PACK)
                 for c0 in (0, HALF):
-                    nc.scalar.activation(
-                        out=x_grouped[:, c0 * PACK : (c0 + HALF) * PACK].rearrange("p (c i t) -> p c t i", i=4, t=PACK),
-                        in_=rows[:, :, c0 : c0 + HALF].rearrange("p t (c i) -> p c t i", i=4),
-                        func=ACT.Abs,
-                    )
+                    weave_x(x_grouped[:, c0 * PACK : (c0 + HALF) * PACK], 0, c0, HALF, 2 * PAIRS)
         quantise_x(x_grouped[:], 0, 0, PAIRS)
         late_tags = ["late0", "x_grouped", "woven0"]
         for k, (c0, width) in enumerate(chunks):

@@ -19,8 +19,19 @@ ACT = mybir.ActivationFunctionType
 P = 128
 PACK = 4
 K_PASS = P * PACK
+QUADRANT = 32
+SCALE_ROWS = 4
 BANK = 512
+BANKS = 8
 HALF = 256
+LIST_ROWS = 16
+RUN = 4
+GAIN_PITCH = 8
+VECTOR_SHARE = 192
+WHOLE_TILES = 6
+LATE_TILES = (6, 7)
+GAIN_ON_GPSIMD = (2, 3)
+CHUNKS = ((0, HALF), (HALF, P), (HALF + P, P))
 
 
 def tile_list_frost_mast_contrast_kernel(
@@ -30,58 +41,59 @@ def tile_list_frost_mast_contrast_kernel(
     with ExitStack() as ctx:
         lists = ctx.enter_context(tc.tile_pool(name="lists", bufs=1))
         keep = ctx.enter_context(tc.tile_pool(name="keep", bufs=1))
-        psum = ctx.enter_context(tc.psum_pool(name="psum", bufs=8))
+        psum = ctx.enter_context(tc.psum_pool(name="psum", bufs=BANKS))
 
         def load_list(src, name):
-            t = lists.tile([P, src.shape[1]], U16, name=name)
-            nc.sync.dma_start(t[:], src)
-            return t
+            tile = lists.tile([P, src.shape[1]], U16, name=name)
+            nc.sync.dma_start(tile[:], src)
+            return tile
 
         offs_sb = load_list(offs, "offs_sb")
         tab_rows = keep.tile([P, T // 4], I32, name="tab_rows", align_bytes=64)
-        tab_sb = []
-        for a in range(2):
-            tab_sb.append(keep.tile([P, T], I32, name="tab_sb%d" % a, align_bytes=64))
+        tab_sb = [keep.tile([P, T], I32, name="tab_sb%d" % a, align_bytes=64) for a in range(2)]
 
         def load_scale_rows(q):
             for a in range(2):
+                row = QUADRANT * q + SCALE_ROWS * a
                 nc.sync.dma_start(
-                    out=tab_rows[32 * q + 4 * a : 32 * q + 4 * a + 4, :],
-                    in_=tab_scales[a, 4 * q : 4 * q + 4, :].bitcast(I32),
+                    out=tab_rows[row : row + SCALE_ROWS, :],
+                    in_=tab_scales[a, SCALE_ROWS * q : SCALE_ROWS * (q + 1), :].bitcast(I32),
                 )
 
         def load_words(a):
             nc.sync.dma_start(out=tab_sb[a][:], in_=tab_words[a].rearrange("p t i -> p (t i)").bitcast(I32))
+
+        raw = {}
+
+        def raw_tag(b, a, c0):
+            return "raw%d%d%d" % (b, a, c0)
+
+        def load_w1(b, a, c0, width):
+            tile = keep.tile([P, PACK, width], F32, name="w1_raw", tag=raw_tag(b, a, c0), align_bytes=64)
+            rows = w1[a * K_PASS : (a + 1) * K_PASS, b * K_PASS + c0 : b * K_PASS + c0 + width]
+            nc.sync.dma_start(out=tile[:], in_=rows.rearrange("(p j) c -> p j c", j=PACK))
+            raw[b, a, c0] = tile
 
         load_scale_rows(0)
         load_scale_rows(2)
         load_scale_rows(1)
         load_words(0)
         load_scale_rows(3)
-
-        raw = {}
-
-        def load_w1(b, a, c0, width):
-            t = keep.tile([P, PACK, width], F32, name="w1_raw", tag="raw%d%d%d" % (b, a, c0), align_bytes=64)
-            rows = w1[a * K_PASS : (a + 1) * K_PASS, b * K_PASS + c0 : b * K_PASS + c0 + width]
-            nc.sync.dma_start(out=t[:], in_=rows.rearrange("(p j) c -> p j c", j=PACK))
-            raw[b, a, c0] = t
-
         load_w1(0, 0, 0, K_PASS)
         load_words(1)
-        pos1_sb = load_list(pos1, "pos1_sb")
-        pos2_sb = load_list(pos2, "pos2_sb")
         load_w1(0, 1, 0, HALF)
         load_w1(0, 1, HALF, HALF)
         load_w1(1, 0, 0, HALF)
+        pos1_sb = load_list(pos1, "pos1_sb")
+        pos2_sb = load_list(pos2, "pos2_sb")
         load_w1(1, 0, HALF, HALF)
         load_w1(1, 1, 0, K_PASS)
-        gain_sb = keep.tile([P, 2, 8], F32, name="gain_sb")
+        gain_sb = keep.tile([P, 2, GAIN_PITCH], F32, name="gain_sb")
         nc.sync.dma_start(out=gain_sb[:, :, 0:PACK], in_=gain.rearrange("(b p t) -> p b t", b=2, t=PACK))
         w4_sb = keep.tile([P, 2 * 2 * N], U8, name="w4_sb", align_bytes=64)
         nc.sync.dma_start(
-            out=w4_sb[:].bitcast(I32).rearrange("p (a c) -> p a c", a=2),
-            in_=w4_words.bitcast(I32).rearrange("a p c -> p a c"),
+            out=w4_sb[:].bitcast(I32).rearrange("p (b c) -> p b c", b=2),
+            in_=w4_words.bitcast(I32).rearrange("b p c -> p b c"),
         )
         pos3_sb = load_list(pos3, "pos3_sb")
         pos4_sb = load_list(pos4, "pos4_sb")
@@ -90,52 +102,51 @@ def tile_list_frost_mast_contrast_kernel(
         tab_plane = keep.tile([P, T], U8, name="tab_plane", align_bytes=64)
         nc.vector.memset(tab_plane[:].bitcast(I32), 0)
         nc.vector.memset(w4_plane[:].bitcast(I32), 0)
-        for q in range(4):
+        for q in range(P // QUADRANT):
+            rows = slice(QUADRANT * q, QUADRANT * q + SCALE_ROWS)
             nc.sync.dma_start(
-                out=w4_plane[32 * q : 32 * q + 4, :].bitcast(I32).rearrange("r (a c) -> r a c", a=2),
-                in_=w4_scales[:, 4 * q : 4 * q + 4, :].bitcast(I32).rearrange("a r c -> r a c"),
+                out=w4_plane[rows, :].bitcast(I32).rearrange("s (b c) -> s b c", b=2),
+                in_=w4_scales[:, SCALE_ROWS * q : SCALE_ROWS * (q + 1), :].bitcast(I32).rearrange("b s c -> s b c"),
             )
-        for q in range(4):
-            nc.vector.tensor_copy(tab_plane[32 * q : 32 * q + 8, :].bitcast(I32), tab_rows[32 * q : 32 * q + 8, :])
+        for q in range(P // QUADRANT):
+            rows = slice(QUADRANT * q, QUADRANT * q + 2 * SCALE_ROWS)
+            nc.vector.tensor_copy(tab_plane[rows, :].bitcast(I32), tab_rows[rows, :])
 
         v_plane = keep.tile([P, S], U8, name="v_plane", align_bytes=64)
         nc.vector.tensor_copy(v_plane[:], tab_plane[:].indirect(offs_sb[:]))
         v_words = []
         for a in range(2):
-            t = keep.tile([P, S], U32, name="v_words%d" % a, align_bytes=64)
-            nc.vector.tensor_copy(t[:], tab_sb[a][:].bitcast(U32).indirect(offs_sb[:]))
-            v_words.append(t)
+            words = keep.tile([P, S], U32, name="v_words%d" % a, align_bytes=64)
+            nc.vector.tensor_copy(words[:], tab_sb[a][:].bitcast(U32).indirect(offs_sb[:]))
+            v_words.append(words)
 
-        grouped, w1_codes, w1_plane = {}, {}, {}
+        rounded, w1_codes, w1_plane = {}, {}, {}
         for b in range(2):
             for a in range(2):
-                grouped[b, a] = keep.tile(
-                    [P, PACK * K_PASS], BF16, name="w1_grouped", tag="grouped%d%d" % (b, a), align_bytes=64
-                )
+                rounded[b, a] = keep.tile([P, PACK * K_PASS], BF16, name="w1_rounded%d%d" % (b, a), align_bytes=64)
                 w1_codes[b, a] = keep.tile([P, K_PASS], U32, name="w1_codes%d%d" % (b, a), align_bytes=64)
                 w1_plane[b, a] = keep.tile([P, K_PASS], U8, name="w1_plane%d%d" % (b, a), align_bytes=64)
 
-        def round_w1(b, a, tile_c0, on_vector, lo=0, hi=HALF):
-            src = raw[b, a, tile_c0][:, :, lo:hi].rearrange("p j (m t) -> p m t j", t=PACK)
-            m0, m1 = (tile_c0 + lo) // PACK, (tile_c0 + hi) // PACK
-            dst = grouped[b, a][:].rearrange("p (t m j) -> p m t j", t=PACK, j=PACK)[:, m0:m1]
-            if on_vector:
-                nc.vector.tensor_copy(out=dst, in_=src)
-            else:
-                nc.scalar.copy(out=dst, in_=src)
+        def round_w1(copy, b, a, c0, lo, hi):
+            src = raw[b, a, c0][:, :, lo:hi].rearrange("p j (m t) -> p m t j", t=PACK)
+            dst = rounded[b, a][:].rearrange("p (t m j) -> p m t j", t=PACK, j=PACK)
+            copy(out=dst[:, (c0 + lo) // PACK : (c0 + hi) // PACK], in_=src)
 
         def quantise_w1(b, a, t0, t1):
             nc.vector.quantize_mx(
                 out=w1_codes[b, a][:, t0 * P : t1 * P].bitcast(FP8X4),
                 scales=w1_plane[b, a][:, t0 * P : t1 * P],
-                in_=grouped[b, a][:, t0 * K_PASS : t1 * K_PASS],
+                in_=rounded[b, a][:, t0 * K_PASS : t1 * K_PASS],
             )
 
-        h = {}
+        tanh_rows = {}
+
+        def tanh_tag(i):
+            return "tanh%d" % i
 
         def first_product(i, tag):
             b, t = divmod(i, PACK)
-            h[i] = keep.tile([P, S], F32, name="h", tag=tag, align_bytes=64)
+            tanh_rows[i] = keep.tile([P, S], F32, name="tanh_rows", tag=tag, align_bytes=64)
             for c0 in range(0, S, BANK):
                 acc = psum.tile([P, BANK], F32, name="acc")
                 for a in range(2):
@@ -144,120 +155,133 @@ def tile_list_frost_mast_contrast_kernel(
                         lhsT=w1_codes[b, a][:, t * P : (t + 1) * P].bitcast(FP8X4),
                         lhsT_scale=w1_plane[b, a][:, t * P : (t + 1) * P],
                         rhs=v_words[a][:, c0 : c0 + BANK].bitcast(FP8X4),
-                        rhs_scale=v_plane[4 * a : P, c0 : c0 + BANK],
+                        rhs_scale=v_plane[SCALE_ROWS * a : P, c0 : c0 + BANK],
                         start=(a == 0),
                         stop=(a == 1),
                     )
-                nc.scalar.activation(out=h[i][:, c0 : c0 + BANK], in_=acc[:], func=ACT.Tanh)
+                nc.scalar.activation(out=tanh_rows[i][:, c0 : c0 + BANK], in_=acc[:], func=ACT.Tanh)
 
-        round_w1(0, 0, 0, False)
-        round_w1(0, 0, 0, False, HALF, K_PASS)
-        quantise_w1(0, 0, 0, 4)
-        round_w1(0, 1, 0, False)
-        round_w1(0, 1, HALF, True, 0, 160)
-        round_w1(0, 1, HALF, False, 160, HALF)
+        on_scalar, on_vector = nc.scalar.copy, nc.vector.tensor_copy
+        round_w1(on_scalar, 0, 0, 0, 0, HALF)
+        round_w1(on_scalar, 0, 0, 0, HALF, K_PASS)
+        quantise_w1(0, 0, 0, PACK)
+        round_w1(on_scalar, 0, 1, 0, 0, HALF)
+        round_w1(on_vector, 0, 1, HALF, 0, VECTOR_SHARE)
+        round_w1(on_scalar, 0, 1, HALF, VECTOR_SHARE, HALF)
         quantise_w1(0, 1, 0, 1)
-        quantise_w1(0, 1, 1, 4)
-        round_w1(1, 0, 0, True)
-        first_product(0, "h0")
-        first_product(1, "h1")
-        round_w1(1, 0, HALF, False)
-        quantise_w1(1, 0, 0, 4)
-        first_product(2, "raw10%d" % HALF)
-        round_w1(1, 1, 0, False)
-        round_w1(1, 1, 0, False, HALF, K_PASS)
-        quantise_w1(1, 1, 0, 4)
-        first_product(3, "raw110")
+        quantise_w1(0, 1, 1, PACK)
+        round_w1(on_vector, 1, 0, 0, 0, HALF)
+        first_product(0, tanh_tag(0))
+        first_product(1, tanh_tag(1))
+        round_w1(on_scalar, 1, 0, HALF, 0, HALF)
+        quantise_w1(1, 0, 0, PACK)
+        first_product(2, raw_tag(1, 0, HALF))
+        round_w1(on_scalar, 1, 1, 0, 0, HALF)
+        round_w1(on_scalar, 1, 1, 0, HALF, K_PASS)
+        quantise_w1(1, 1, 0, PACK)
+        first_product(3, raw_tag(1, 1, 0))
         for i in (4, 6, 5, 7):
-            first_product(i, "h%d" % i)
+            first_product(i, tanh_tag(i))
 
-        chunks = [(0, HALF), (HALF, P), (HALF + P, P)]
-        upper = 2 * PAIRS + chunks[-1][0]
+        late_place = 2 * PAIRS + CHUNKS[-1][0]
         x_rows = {}
         x_codes = [keep.tile([P, PAIRS], U32, name="x_codes%d" % b, align_bytes=64) for b in range(2)]
         x_plane = [keep.tile([P, PAIRS], U8, name="x_plane%d" % b, align_bytes=64) for b in range(2)]
 
-        def two_differences(steps):
-            firsts = []
-            for i, c0, width, dst in steps:
-                first = keep.tile([P, HALF], F32, name="first", tag="h%d" % (11 - i), align_bytes=64)
-                nc.vector.tensor_copy(first[:, 0:width], h[i][:].indirect(pos1_sb[:, c0 // 16 : (c0 + width) // 16]))
-                firsts.append(first)
-            for first, (i, c0, width, dst) in zip(firsts, steps):
-                nc.vector.tensor_tensor(
-                    dst, h[i][:].indirect(pos2_sb[:, c0 // 16 : (c0 + width) // 16]), first[:, 0:width], ALU.subtract
-                )
-
-        def scale_abs(dst, src, i):
+        def gain_of(i):
             b, t = divmod(i, PACK)
-            nc.scalar.activation(out=dst, in_=src, func=ACT.Abs, scale=gain_sb[:, b, t : t + 1])
+            return gain_sb[:, b, t : t + 1]
 
-        def weave_x(dst, b, c0, width, pitch, copy=nc.scalar.copy):
-            rows = x_rows[b][:, c0 : c0 + 2 * pitch].rearrange("p (u r) -> p u r", u=2)[:, :, 0 : 2 * PAIRS]
-            src = rows.rearrange("p u (l m) -> p u l m", l=2)[:, :, :, 0:width].rearrange("p u l (c i) -> p c u l i", i=4)
-            copy(out=dst.rearrange("p (c i u l) -> p c u l i", i=4, u=2, l=2), in_=src)
-
-        def quantise_x(src, b, c0, width):
+        def quantise_x(woven, b, c0, width):
             nc.vector.quantize_mx(
-                out=x_codes[b][:, c0 : c0 + width].bitcast(FP8X4), scales=x_plane[b][:, c0 : c0 + width], in_=src
+                out=x_codes[b][:, c0 : c0 + width].bitcast(FP8X4), scales=x_plane[b][:, c0 : c0 + width], in_=woven
             )
 
-        x_grouped = keep.tile([P, PAIRS * PACK], BF16, name="x_grouped", tag="x_grouped", align_bytes=64)
-        for i in range(6):
+        woven_first = keep.tile([P, PAIRS * PACK], BF16, name="woven_first", tag="woven_first", align_bytes=64)
+        for i in range(WHOLE_TILES):
             b, t = divmod(i, PACK)
             if t == 0:
-                x_rows[b] = keep.tile([P, 2 * upper], F32, name="x_rows", tag="x_rows", align_bytes=64)
+                x_rows[b] = keep.tile([P, 2 * late_place], F32, name="x_rows", tag="x_rows", align_bytes=64)
             diff = keep.tile([P, PAIRS], F32, name="diff%d" % i)
             picked = []
-            for which, pos in enumerate((pos1_sb, pos2_sb)):
-                tag = "picked%d%d" % (i, which)
-                picked.append(keep.tile([P, PAIRS], F32, name="picked", tag=tag, align_bytes=64))
-                nc.vector.tensor_copy(picked[which][:], h[i][:].indirect(pos[:]))
+            for which, pos_sb in enumerate((pos1_sb, pos2_sb)):
+                picked.append(keep.tile([P, PAIRS], F32, name="picked%d%d" % (i, which), align_bytes=64))
+                nc.vector.tensor_copy(picked[which][:], tanh_rows[i][:].indirect(pos_sb[:]))
             nc.gpsimd.tensor_tensor(diff[:], picked[0][:], picked[1][:], ALU.subtract)
             row = x_rows[b][:, t * PAIRS : (t + 1) * PAIRS]
-            scale_abs(row, diff[:], i)
+            if i in GAIN_ON_GPSIMD:
+                nc.gpsimd.tensor_scalar(row, diff[:], gain_of(i), 0.0, ALU.mult, ALU.add)
+            else:
+                nc.scalar.activation(out=row, in_=diff[:], func=ACT.Abs, scale=gain_of(i))
             if i == PACK - 1:
+                rows = x_rows[0][:, 0 : PACK * PAIRS].rearrange("p (t m) -> p t m", t=PACK)
                 for c0 in (0, HALF):
-                    weave_x(x_grouped[:, c0 * PACK : (c0 + HALF) * PACK], 0, c0, HALF, 2 * PAIRS)
-        quantise_x(x_grouped[:], 0, 0, PAIRS)
-        late_tags = ["late0", "x_grouped", "woven0"]
-        for k, (c0, width) in enumerate(chunks):
-            pair = keep.tile([P, 2 * width], F32, name="late", tag=late_tags[k], align_bytes=64)
-            late = {i: pair[:, (i - 6) * width : (i - 5) * width] for i in (6, 7)}
-            two_differences([(i, c0, width, late[i]) for i in (6, 7)])
-            for i in (6, 7):
-                row = upper + (i - 6) * PAIRS
-                scale_abs(x_rows[1][:, row : row + width], late[i], i)
+                    dst = woven_first[:, c0 * PACK : (c0 + HALF) * PACK]
+                    nc.scalar.activation(
+                        out=dst.rearrange("p (c i t) -> p c t i", i=RUN, t=PACK),
+                        in_=rows[:, :, c0 : c0 + HALF].rearrange("p t (c i) -> p c t i", i=RUN),
+                        func=ACT.Abs,
+                    )
+        quantise_x(woven_first[:], 0, 0, PAIRS)
+
+        diff_tags = ("late_diff", "woven_first", "woven0")
+        for k, (c0, width) in enumerate(CHUNKS):
+            entries = slice(c0 // LIST_ROWS, (c0 + width) // LIST_ROWS)
+            late_diff = keep.tile([P, 2 * width], F32, name="late_diff", tag=diff_tags[k], align_bytes=64)
+            firsts = []
+            for i, done in zip(LATE_TILES, (5, 4)):
+                first = keep.tile([P, HALF], F32, name="first", tag=tanh_tag(done), align_bytes=64)
+                nc.vector.tensor_copy(first[:, 0:width], tanh_rows[i][:].indirect(pos1_sb[:, entries]))
+                firsts.append(first)
+            for u, i in enumerate(LATE_TILES):
+                nc.vector.tensor_tensor(
+                    late_diff[:, u * width : (u + 1) * width],
+                    tanh_rows[i][:].indirect(pos2_sb[:, entries]),
+                    firsts[u][:, 0:width],
+                    ALU.subtract,
+                )
+            for u, i in enumerate(LATE_TILES):
+                nc.scalar.activation(
+                    out=x_rows[1][:, late_place + u * PAIRS : late_place + u * PAIRS + width],
+                    in_=late_diff[:, u * width : (u + 1) * width],
+                    func=ACT.Abs,
+                    scale=gain_of(i),
+                )
             woven = keep.tile([P, width * PACK], BF16, name="woven", tag="woven%d" % k, align_bytes=64)
-            weave_x(woven[:], 1, c0, width, upper - c0, nc.vector.tensor_copy if k == len(chunks) - 1 else nc.scalar.copy)
+            pitch = late_place - c0
+            src = x_rows[1][:, c0 : c0 + 2 * pitch].rearrange("p (upper r) -> p upper r", upper=2)[:, :, 0 : 2 * PAIRS]
+            src = src.rearrange("p upper (lower m) -> p upper lower m", lower=2)[:, :, :, 0:width]
+            weave = on_vector if k == len(CHUNKS) - 1 else on_scalar
+            weave(
+                out=woven[:].rearrange("p (c i upper lower) -> p c upper lower i", i=RUN, upper=2, lower=2),
+                in_=src.rearrange("p upper lower (c i) -> p c upper lower i", i=RUN),
+            )
             quantise_x(woven[:], 1, c0, width)
 
-        def second_pass(acc, n, b, c0, width, start, stop):
-            nc.tensor.matmul_mx(
-                out=acc,
-                lhsT=w4_sb[:, 2 * (b * N + n * P) : 2 * (b * N + (n + 1) * P)].bitcast(FP4X4),
-                lhsT_scale=w4_plane[:, b * N + n * P : b * N + (n + 1) * P],
-                rhs=x_codes[b][:, c0 : c0 + width].bitcast(FP8X4),
-                rhs_scale=x_plane[b][:, c0 : c0 + width],
-                start=start,
-                stop=stop,
-            )
+        def second_product(y, n, pieces):
+            acc = psum.tile([P, BANK], F32, name="acc")
+            passes = [(b, c0, width) for b in range(2) for c0, width in pieces]
+            for k, (b, c0, width) in enumerate(passes):
+                col = b * N + n * P
+                nc.tensor.matmul_mx(
+                    out=acc[:, c0 : c0 + width],
+                    lhsT=w4_sb[:, 2 * col : 2 * (col + P)].bitcast(FP4X4),
+                    lhsT_scale=w4_plane[:, col : col + P],
+                    rhs=x_codes[b][:, c0 : c0 + width].bitcast(FP8X4),
+                    rhs_scale=x_plane[b][:, c0 : c0 + width],
+                    start=(k == 0),
+                    stop=(k == len(passes) - 1),
+                )
+            lo, hi = pieces[0][0], pieces[-1][0] + pieces[-1][1]
+            nc.scalar.copy(out=y[:, lo:hi], in_=acc[:, lo:hi])
 
         for n in range(N // P):
             y = keep.tile([P, PAIRS], F32, name="y%d" % n)
             if n == 0:
-                for part in (chunks[:-1], chunks[-1:]):
-                    acc = psum.tile([P, BANK], F32, name="acc")
-                    passes = [(b, c0, width) for b in range(2) for c0, width in part]
-                    for k, (b, c0, width) in enumerate(passes):
-                        second_pass(acc[:, c0 : c0 + width], n, b, c0, width, k == 0, k == len(passes) - 1)
-                    lo, hi = part[0][0], part[-1][0] + part[-1][1]
-                    nc.scalar.copy(out=y[:, lo:hi], in_=acc[:, lo:hi])
+                second_product(y, n, CHUNKS[:-1])
+                second_product(y, n, CHUNKS[-1:])
             else:
-                acc = psum.tile([P, BANK], F32, name="acc")
-                second_pass(acc[:], n, 0, 0, PAIRS, True, False)
-                second_pass(acc[:], n, 1, 0, PAIRS, False, True)
-                nc.scalar.copy(out=y[:], in_=acc[:])
+                second_product(y, n, ((0, PAIRS),))
             rival_a = keep.tile([P, RIVALS], F32, name="rival_a%d" % n)
             rival_b = keep.tile([P, RIVALS], F32, name="rival_b%d" % n)
             best = keep.tile([P, RIVALS], F32, name="best%d" % n)

from contextlib import ExitStack

import concourse.mybir as mybir

K, H, N, T, S, PAIRS, RIVALS = 1024, 1024, 512, 4096, 1024, 512, 256
FLOPS = 2 * K * H * S + 2 * H * N * PAIRS

F32 = mybir.dt.float32
BF16 = mybir.dt.bfloat16
I32 = mybir.dt.int32
U32 = mybir.dt.uint32
U16 = mybir.dt.uint16
U8 = mybir.dt.uint8
FP8X4 = mybir.dt.float8_e4m3fn_x4
FP4X4 = mybir.dt.float4_e2m1fn_x4
ALU = mybir.AluOpType
ACT = mybir.ActivationFunctionType

P = 128
PACK = 4
K_PASS = P * PACK
QUADRANT = 32
SCALE_ROWS = 4
BANK = 512
BANKS = 8
HALF = 256
LIST_ROWS = 16
RUN = 4
GAIN_PITCH = 8
VECTOR_SHARE = 192
WHOLE_TILES = 6
LATE_TILES = (6, 7)
GAIN_ON_GPSIMD = (2, 3)
CHUNKS = ((0, HALF), (HALF, P), (HALF + P, P))


def tile_list_frost_mast_contrast_kernel(
    tc, tab_words, tab_scales, offs, w1, gain, pos1, pos2, w4_words, w4_scales, pos3, pos4, out
):
    nc = tc.nc
    with ExitStack() as ctx:
        lists = ctx.enter_context(tc.tile_pool(name="lists", bufs=1))
        keep = ctx.enter_context(tc.tile_pool(name="keep", bufs=1))
        psum = ctx.enter_context(tc.psum_pool(name="psum", bufs=BANKS))

        def load_list(src, name):
            tile = lists.tile([P, src.shape[1]], U16, name=name)
            nc.sync.dma_start(tile[:], src)
            return tile

        offs_sb = load_list(offs, "offs_sb")
        tab_rows = keep.tile([P, T // 4], I32, name="tab_rows", align_bytes=64)
        tab_sb = [keep.tile([P, T], I32, name="tab_sb%d" % a, align_bytes=64) for a in range(2)]

        def load_scale_rows(q):
            for a in range(2):
                row = QUADRANT * q + SCALE_ROWS * a
                nc.sync.dma_start(
                    out=tab_rows[row : row + SCALE_ROWS, :],
                    in_=tab_scales[a, SCALE_ROWS * q : SCALE_ROWS * (q + 1), :].bitcast(I32),
                )

        def load_words(a):
            nc.sync.dma_start(out=tab_sb[a][:], in_=tab_words[a].rearrange("p t i -> p (t i)").bitcast(I32))

        raw = {}

        def raw_tag(b, a, c0):
            return "raw%d%d%d" % (b, a, c0)

        def load_w1(b, a, c0, width):
            tile = keep.tile([P, PACK, width], F32, name="w1_raw", tag=raw_tag(b, a, c0), align_bytes=64)
            rows = w1[a * K_PASS : (a + 1) * K_PASS, b * K_PASS + c0 : b * K_PASS + c0 + width]
            nc.sync.dma_start(out=tile[:], in_=rows.rearrange("(p j) c -> p j c", j=PACK))
            raw[b, a, c0] = tile

        load_scale_rows(0)
        load_scale_rows(2)
        load_scale_rows(1)
        load_words(0)
        load_scale_rows(3)
        load_w1(0, 0, 0, K_PASS)
        load_words(1)
        load_w1(0, 1, 0, HALF)
        load_w1(0, 1, HALF, HALF)
        load_w1(1, 0, 0, HALF)
        pos1_sb = load_list(pos1, "pos1_sb")
        pos2_sb = load_list(pos2, "pos2_sb")
        load_w1(1, 0, HALF, HALF)
        load_w1(1, 1, 0, K_PASS)
        gain_sb = keep.tile([P, 2, GAIN_PITCH], F32, name="gain_sb")
        nc.sync.dma_start(out=gain_sb[:, :, 0:PACK], in_=gain.rearrange("(b p t) -> p b t", b=2, t=PACK))
        w4_sb = keep.tile([P, 2 * 2 * N], U8, name="w4_sb", align_bytes=64)
        nc.sync.dma_start(
            out=w4_sb[:].bitcast(I32).rearrange("p (b c) -> p b c", b=2),
            in_=w4_words.bitcast(I32).rearrange("b p c -> p b c"),
        )
        pos3_sb = load_list(pos3, "pos3_sb")
        pos4_sb = load_list(pos4, "pos4_sb")

        w4_plane = keep.tile([P, 2 * N], U8, name="w4_plane", align_bytes=64)
        tab_plane = keep.tile([P, T], U8, name="tab_plane", align_bytes=64)
        nc.vector.memset(tab_plane[:].bitcast(I32), 0)
        nc.vector.memset(w4_plane[:].bitcast(I32), 0)
        for q in range(P // QUADRANT):
            rows = slice(QUADRANT * q, QUADRANT * q + SCALE_ROWS)
            nc.sync.dma_start(
                out=w4_plane[rows, :].bitcast(I32).rearrange("s (b c) -> s b c", b=2),
                in_=w4_scales[:, SCALE_ROWS * q : SCALE_ROWS * (q + 1), :].bitcast(I32).rearrange("b s c -> s b c"),
            )
        for q in range(P // QUADRANT):
            rows = slice(QUADRANT * q, QUADRANT * q + 2 * SCALE_ROWS)
            nc.vector.tensor_copy(tab_plane[rows, :].bitcast(I32), tab_rows[rows, :])

        v_plane = keep.tile([P, S], U8, name="v_plane", align_bytes=64)
        nc.vector.tensor_copy(v_plane[:], tab_plane[:].indirect(offs_sb[:]))
        v_words = []
        for a in range(2):
            words = keep.tile([P, S], U32, name="v_words%d" % a, align_bytes=64)
            nc.vector.tensor_copy(words[:], tab_sb[a][:].bitcast(U32).indirect(offs_sb[:]))
            v_words.append(words)

        rounded, w1_codes, w1_plane = {}, {}, {}
        for b in range(2):
            for a in range(2):
                rounded[b, a] = keep.tile([P, PACK * K_PASS], BF16, name="w1_rounded%d%d" % (b, a), align_bytes=64)
                w1_codes[b, a] = keep.tile([P, K_PASS], U32, name="w1_codes%d%d" % (b, a), align_bytes=64)
                w1_plane[b, a] = keep.tile([P, K_PASS], U8, name="w1_plane%d%d" % (b, a), align_bytes=64)

        def round_w1(copy, b, a, c0, lo, hi):
            src = raw[b, a, c0][:, :, lo:hi].rearrange("p j (m t) -> p m t j", t=PACK)
            dst = rounded[b, a][:].rearrange("p (t m j) -> p m t j", t=PACK, j=PACK)
            copy(out=dst[:, (c0 + lo) // PACK : (c0 + hi) // PACK], in_=src)

        def quantise_w1(b, a, t0, t1):
            nc.vector.quantize_mx(
                out=w1_codes[b, a][:, t0 * P : t1 * P].bitcast(FP8X4),
                scales=w1_plane[b, a][:, t0 * P : t1 * P],
                in_=rounded[b, a][:, t0 * K_PASS : t1 * K_PASS],
            )

        tanh_rows = {}

        def tanh_tag(i):
            return "tanh%d" % i

        def first_product(i, tag):
            b, t = divmod(i, PACK)
            tanh_rows[i] = keep.tile([P, S], F32, name="tanh_rows", tag=tag, align_bytes=64)
            for c0 in range(0, S, BANK):
                acc = psum.tile([P, BANK], F32, name="acc")
                for a in range(2):
                    nc.tensor.matmul_mx(
                        out=acc[:],
                        lhsT=w1_codes[b, a][:, t * P : (t + 1) * P].bitcast(FP8X4),
                        lhsT_scale=w1_plane[b, a][:, t * P : (t + 1) * P],
                        rhs=v_words[a][:, c0 : c0 + BANK].bitcast(FP8X4),
                        rhs_scale=v_plane[SCALE_ROWS * a : P, c0 : c0 + BANK],
                        start=(a == 0),
                        stop=(a == 1),
                    )
                nc.scalar.activation(out=tanh_rows[i][:, c0 : c0 + BANK], in_=acc[:], func=ACT.Tanh)

        on_scalar, on_vector = nc.scalar.copy, nc.vector.tensor_copy
        round_w1(on_scalar, 0, 0, 0, 0, HALF)
        round_w1(on_scalar, 0, 0, 0, HALF, K_PASS)
        quantise_w1(0, 0, 0, PACK)
        round_w1(on_scalar, 0, 1, 0, 0, HALF)
        round_w1(on_vector, 0, 1, HALF, 0, VECTOR_SHARE)
        round_w1(on_scalar, 0, 1, HALF, VECTOR_SHARE, HALF)
        quantise_w1(0, 1, 0, 1)
        quantise_w1(0, 1, 1, PACK)
        round_w1(on_vector, 1, 0, 0, 0, HALF)
        first_product(0, tanh_tag(0))
        first_product(1, tanh_tag(1))
        round_w1(on_scalar, 1, 0, HALF, 0, HALF)
        quantise_w1(1, 0, 0, PACK)
        first_product(2, raw_tag(1, 0, HALF))
        round_w1(on_scalar, 1, 1, 0, 0, HALF)
        round_w1(on_scalar, 1, 1, 0, HALF, K_PASS)
        quantise_w1(1, 1, 0, PACK)
        first_product(3, raw_tag(1, 1, 0))
        for i in (4, 6, 5, 7):
            first_product(i, tanh_tag(i))

        late_place = 2 * PAIRS + CHUNKS[-1][0]
        x_rows = {}
        x_codes = [keep.tile([P, PAIRS], U32, name="x_codes%d" % b, align_bytes=64) for b in range(2)]
        x_plane = [keep.tile([P, PAIRS], U8, name="x_plane%d" % b, align_bytes=64) for b in range(2)]

        def gain_of(i):
            b, t = divmod(i, PACK)
            return gain_sb[:, b, t : t + 1]

        def quantise_x(woven, b, c0, width):
            nc.vector.quantize_mx(
                out=x_codes[b][:, c0 : c0 + width].bitcast(FP8X4), scales=x_plane[b][:, c0 : c0 + width], in_=woven
            )

        woven_first = keep.tile([P, PAIRS * PACK], BF16, name="woven_first", tag="woven_first", align_bytes=64)
        for i in range(WHOLE_TILES):
            b, t = divmod(i, PACK)
            if t == 0:
                x_rows[b] = keep.tile([P, 2 * late_place], F32, name="x_rows", tag="x_rows", align_bytes=64)
            diff = keep.tile([P, PAIRS], F32, name="diff%d" % i)
            picked = []
            for which, pos_sb in enumerate((pos1_sb, pos2_sb)):
                picked.append(keep.tile([P, PAIRS], F32, name="picked%d%d" % (i, which), align_bytes=64))
                nc.vector.tensor_copy(picked[which][:], tanh_rows[i][:].indirect(pos_sb[:]))
            nc.gpsimd.tensor_tensor(diff[:], picked[0][:], picked[1][:], ALU.subtract)
            row = x_rows[b][:, t * PAIRS : (t + 1) * PAIRS]
            if i in GAIN_ON_GPSIMD:
                nc.gpsimd.tensor_scalar(row, diff[:], gain_of(i), 0.0, ALU.mult, ALU.add)
            else:
                nc.scalar.activation(out=row, in_=diff[:], func=ACT.Abs, scale=gain_of(i))
            if i == PACK - 1:
                rows = x_rows[0][:, 0 : PACK * PAIRS].rearrange("p (t m) -> p t m", t=PACK)
                for c0 in (0, HALF):
                    dst = woven_first[:, c0 * PACK : (c0 + HALF) * PACK]
                    nc.scalar.activation(
                        out=dst.rearrange("p (c i t) -> p c t i", i=RUN, t=PACK),
                        in_=rows[:, :, c0 : c0 + HALF].rearrange("p t (c i) -> p c t i", i=RUN),
                        func=ACT.Abs,
                    )
        quantise_x(woven_first[:], 0, 0, PAIRS)

        diff_tags = ("late_diff", "woven_first", "woven0")
        for k, (c0, width) in enumerate(CHUNKS):
            entries = slice(c0 // LIST_ROWS, (c0 + width) // LIST_ROWS)
            late_diff = keep.tile([P, 2 * width], F32, name="late_diff", tag=diff_tags[k], align_bytes=64)
            firsts = []
            for i, done in zip(LATE_TILES, (5, 4)):
                first = keep.tile([P, HALF], F32, name="first", tag=tanh_tag(done), align_bytes=64)
                nc.vector.tensor_copy(first[:, 0:width], tanh_rows[i][:].indirect(pos1_sb[:, entries]))
                firsts.append(first)
            for u, i in enumerate(LATE_TILES):
                nc.vector.tensor_tensor(
                    late_diff[:, u * width : (u + 1) * width],
                    tanh_rows[i][:].indirect(pos2_sb[:, entries]),
                    firsts[u][:, 0:width],
                    ALU.subtract,
                )
            for u, i in enumerate(LATE_TILES):
                nc.scalar.activation(
                    out=x_rows[1][:, late_place + u * PAIRS : late_place + u * PAIRS + width],
                    in_=late_diff[:, u * width : (u + 1) * width],
                    func=ACT.Abs,
                    scale=gain_of(i),
                )
            woven = keep.tile([P, width * PACK], BF16, name="woven", tag="woven%d" % k, align_bytes=64)
            pitch = late_place - c0
            src = x_rows[1][:, c0 : c0 + 2 * pitch].rearrange("p (upper r) -> p upper r", upper=2)[:, :, 0 : 2 * PAIRS]
            src = src.rearrange("p upper (lower m) -> p upper lower m", lower=2)[:, :, :, 0:width]
            weave = on_vector if k == len(CHUNKS) - 1 else on_scalar
            weave(
                out=woven[:].rearrange("p (c i upper lower) -> p c upper lower i", i=RUN, upper=2, lower=2),
                in_=src.rearrange("p upper lower (c i) -> p c upper lower i", i=RUN),
            )
            quantise_x(woven[:], 1, c0, width)

        def second_product(y, n, pieces):
            acc = psum.tile([P, BANK], F32, name="acc")
            passes = [(b, c0, width) for b in range(2) for c0, width in pieces]
            for k, (b, c0, width) in enumerate(passes):
                col = b * N + n * P
                nc.tensor.matmul_mx(
                    out=acc[:, c0 : c0 + width],
                    lhsT=w4_sb[:, 2 * col : 2 * (col + P)].bitcast(FP4X4),
                    lhsT_scale=w4_plane[:, col : col + P],
                    rhs=x_codes[b][:, c0 : c0 + width].bitcast(FP8X4),
                    rhs_scale=x_plane[b][:, c0 : c0 + width],
                    start=(k == 0),
                    stop=(k == len(passes) - 1),
                )
            lo, hi = pieces[0][0], pieces[-1][0] + pieces[-1][1]
            nc.scalar.copy(out=y[:, lo:hi], in_=acc[:, lo:hi])

        for n in range(N // P):
            y = keep.tile([P, PAIRS], F32, name="y%d" % n)
            if n == 0:
                second_product(y, n, CHUNKS[:-1])
                second_product(y, n, CHUNKS[-1:])
            else:
                second_product(y, n, ((0, PAIRS),))
            rival_a = keep.tile([P, RIVALS], F32, name="rival_a%d" % n)
            rival_b = keep.tile([P, RIVALS], F32, name="rival_b%d" % n)
            best = keep.tile([P, RIVALS], F32, name="best%d" % n)
            nc.vector.tensor_copy(rival_a[:], y[:].indirect(pos3_sb[:]))
            nc.vector.tensor_copy(rival_b[:], y[:].indirect(pos4_sb[:]))
            nc.vector.tensor_tensor(best[:], rival_a[:], rival_b[:], ALU.max)
            nc.sync.dma_start(out=out[n * P : (n + 1) * P, :], in_=best[:])
